import numpy as np, ml_dtypes
CORES = [16,18,20,22]
N = 4
import mx_ref
BF = ml_dtypes.bfloat16
def entries(a):
    return np.ascontiguousarray(a.T).reshape(-1)
def table(e):
    return np.ascontiguousarray(np.reshape(e, (-1, 16)).T).astype(np.int32)
def cut(t, i, w=512):
    return t[:, w * i:w * i + w]
def f(rng, *shape):
    return mx_ref.flush((rng.standard_normal(shape, dtype=np.float32) * np.exp2(rng.integers(-2, 3, shape[:-1] + (1,)))).astype(BF))
def wide(rng, *shape, cols=0):
    v = rng.standard_normal(shape, dtype=np.float32) * np.exp2(rng.integers(-12, 13, shape)).astype(np.float32)
    if cols: v *= np.repeat(np.exp2(rng.integers(-cols, cols + 1, shape[:-2] + (1, shape[-1] // 4))) * (rng.random(shape[:-2] + (1, shape[-1] // 4)) > 0.0625), 4, axis=-1).astype(np.float32)
    return mx_ref.flush(v.astype(BF))
SH, CH, R = 256, 64, 3
def lists(rng, how=""):
    o = []
    for q in range(N):
        p = rng.permutation(SH); h = int(rng.integers(0, 2)); e = []
        for t in range(R):
            if how == "same": v = p[:CH]
            elif how == "apart": v = p[CH * t:CH * t + CH]
            elif how == "ends": v = np.arange(CH) + (SH - CH) * ((h + t) % 2)
            elif how == "pairs": v = p[CH:2 * CH] if t >= 2 - h else p[:CH]
            else: v = rng.permutation(SH)[:CH]
            e.append(rng.permutation(v))
        o.append(table(np.concatenate(e)))
    return np.stack(o)
def fit(v):
    v = np.array(v); v[np.abs(v.astype(np.float32)) < np.float32(2.0 ** -30)] = 0
    return v
def setup_inputs(rng):
    return {"x": f(rng, N, 128, 512 * (R + 1)), "wm": f(rng, N, 128, 4 * SH), "dl": f(rng, N, 128, 4 * R * CH), "ix": lists(rng)}
def setup_inputs_same(rng):
    d = setup_inputs(rng); d["ix"] = lists(rng, "same"); return d
def setup_inputs_apart(rng):
    d = setup_inputs(rng); d["ix"] = lists(rng, "apart"); return d
def setup_inputs_ends(rng):
    d = setup_inputs(rng); d["ix"] = lists(rng, "ends"); return d
def setup_inputs_pairs(rng):
    d = setup_inputs(rng); d["ix"] = lists(rng, "pairs"); return d
def setup_inputs_spread(rng):
    d = setup_inputs(rng); d["wm"] = fit(wide(rng, N, 128, 4 * SH, cols=6)); d["dl"] = fit(wide(rng, N, 128, 4 * R * CH, cols=6)); return d
def check_inputs(d):
    b = []
    for n in ("x", "wm", "dl"):
        v = np.abs(np.asarray(d[n]).astype(np.float32))
        if not np.isfinite(v).all() or ((v > 0) & ((v < 2.0 ** -30) | (v > 2.0 ** 30))).any(): b.append(n)
    for q in range(N):
        e = entries(d["ix"][q])
        if e.min() < 0 or e.max() >= SH or any(len(set(e[CH * t:CH * t + CH].tolist())) != CH for t in range(R)): b.append("ix")
    return b
def reference(x, wm, dl, ix):
    X = [[mx_ref.quantize(np.ascontiguousarray(cut(x[r], t))) for t in range(R + 1)] for r in range(N)]
    y = np.zeros((N, 128, (R + 1) * N * SH), np.float32)
    for q in range(N):
        W = np.array(wm[q]).reshape(128, SH, 4); new = np.array(dl[q]).reshape(128, R * CH, 4); e = entries(ix[q])
        for t in range(R + 1):
            if t: W[:, e[CH * (t - 1):CH * t]] = new[:, CH * (t - 1):CH * t]
            held = mx_ref.quantize(np.array(W).reshape(128, 4 * SH)); k = SH * (t * N + q)
            for r in range(N): y[r][:, k:k + SH] = mx_ref.matmul(X[r][t], held)
    return {"y": y}

@@ -1,0 +1,287 @@
+from concourse.bass import DstId, RemoteDMATransfer
+from concourse.mybir import dt, AluOpType, ActivationFunctionType
+
+N, SH, CH, R = 4, 256, 64, 3
+NEW = R * CH
+HELD = SH + NEW
+SEG = SH + 32
+LOW = -8192.0
+
+SCRATCH = {
+    "wmt": ("sbuf", [128, 4 * SH], "bfloat16"),
+    "dlt": ("sbuf", [128, 4 * NEW], "bfloat16"),
+    "xt": ("sbuf", [128, 512 * (R + 1)], "bfloat16"),
+    "xq": ("sbuf", [128, 512], "float8_e4m3fn_x4"),
+    "xsc": ("sbuf", [128, 512], "uint8"),
+    "lst": ("sbuf", [128, 12], "int32"),
+    "off": ("sbuf", [128, 12], "uint16"),
+    "vals": ("sbuf", [128, NEW], "bfloat16"),
+    "row": ("sbuf", [128, R * SEG], "bfloat16"),
+    "tr": ("sbuf", [128, R * SEG], "bfloat16"),
+    "pi": ("sbuf", [128, 2], "int32"),
+    "pk": ("sbuf", [128, 16], "int32"),
+    "si": ("sbuf", [128, 2], "int32"),
+    "hi": ("sbuf", [128, 2], "int32"),
+    "odd": ("sbuf", [128, 2], "float32"),
+    "even": ("sbuf", [128, 2], "float32"),
+    "pos": ("sbuf", [128, 6], "float32"),
+    "hf": ("sbuf", [128, 2], "float32"),
+    "ident": ("sbuf", [128, 16], "float32"),
+    "pa": ("sbuf", [128, 54], "float32"),
+    "pb": ("sbuf", [128, 54], "float32"),
+    "gg": ("sbuf", [128, 52], "float32"),
+    "mt": ("sbuf", [128, 48], "float32"),
+    "tdram": ("dram", [128, 4], "uint16"),
+}
+for _q in range(N):
+    SCRATCH["win%d" % _q] = ("sbuf", [128, HELD], "float8_e4m3fn_x4")
+    SCRATCH["scl%d" % _q] = ("sbuf", [128, HELD], "uint8")
+    SCRATCH["tab%d" % _q] = ("sbuf", [128, 48], "uint16")
+    SCRATCH["ld%d" % _q] = ("dram", [128, 4], "uint16")
+for _h in range(2):
+    for _t in range(R + 1):
+        SCRATCH["y%d%d" % (_h, _t)] = ("sbuf", [128, 512], "float32")
+        if _t:
+            SCRATCH["wc%d%d" % (_h, _t)] = ("sbuf", [128, 512], "float8_e4m3fn_x4")
+            SCRATCH["ws%d%d" % (_h, _t)] = ("sbuf", [128, 512], "uint8")
+for _b in range(8):
+    SCRATCH["ps%d" % _b] = ("psum", [128, 512], "float32")
+
+SEMAPHORES = ["sv", "ss", "st", "sg", "lix", "lwm", "ldl", "lx0", "lx1", "tdr", "ysem", "ls"]
+for _q in range(N):
+    SEMAPHORES += ["ac%d" % _q, "as%d" % _q, "at%d" % _q, "ad%d" % _q, "tl%d" % _q]
+
+
+def rank_program(g, core, T, topo):
+    r = T.rank_of(core)
+    if r is None:
+        return
+    A = AluOpType
+    COPY = ActivationFunctionType.Copy
+    queues = {"v": g.vector, "s": g.scalar, "t": g.tensor, "g": g, "y": g.sync}
+    count = {}
+    ev = {}
+    seen = {}
+
+    def after(qn, *names):
+        for n in names:
+            sem, val = ev[n]
+            if seen.get((qn, sem), 0) < val:
+                queues[qn].wait_ge(T.sem[sem], val)
+                seen[(qn, sem)] = val
+
+    def did(ins, sem, name, n=1):
+        count[sem] = count.get(sem, 0) + n
+        ins.then_inc(T.sem[sem], n)
+        ev[name] = (sem, count[sem])
+
+    mine = [q for q in range(N) if topo.die(T.cores[q]) == topo.die(core)]
+    other = [q for q in range(N) if q not in mine]
+    near = [q for q in mine if q != r][0]
+    i = mine.index(r)
+    far1, far2 = other[i], other[1 - i]
+    peers = [near, far1, far2]
+    hh, fh = r // 2, far1 // 2
+    for q in peers:
+        ev["codes%d" % q] = ("ac%d" % q, 16)
+        ev["scales%d" % q] = ("as%d" % q, 16)
+        ev["tab%d_1" % q] = ("at%d" % q, 16)
+        for t in (2, 3):
+            ev["tab%d_%d" % (q, t)] = ("at%d" % q, 16) if q == near else ("tl%d" % q, 128)
+        ev["ld%d" % q] = ("ad%d" % q, 16)
+
+    nls = [0]
+
+    def send(src, dst, sem, dsts):
+        ids = []
+        for q in dsts:
+            rid, pid, _ = topo.addr(T.cores[q])
+            ids.append(DstId(rid=rid, pnc=pid))
+        m = topo.mask(core, T.cores[dsts[0]])
+        g.remote_dma_fused([RemoteDMATransfer(dst_ids=ids, dma_engine_mask=m, remote_sem=T.sem[sem], srcs=[src],
+                                              dsts=[dst for _ in dsts])], local_sem=T.sem["ls"])
+        nls[0] += len(topo.engines(core, T.cores[dsts[0]]))
+
+    def send_codes(q, dsts):
+        after("g", "codes%d" % q)
+        w = T["win%d" % q][:].bitcast(dt.uint8)
+        send(w, w, "ac%d" % q, dsts)
+
+    def send_scales(q, dsts):
+        after("g", "scales%d" % q)
+        w = T["scl%d" % q][:]
+        send(w, w, "as%d" % q, dsts)
+
+    win, scl, tab = T["win%d" % r], T["scl%d" % r], T["tab%d" % r]
+    v = g.vector
+
+    for k in range(4):
+        g.sync.dma_start(T.lst[16 * k:16 * k + 16, :], T.ix[:]).then_inc(T.sem["lix"], 16)
+        g.scalar.dma_start(T.lst[64 + 16 * k:80 + 16 * k, :], T.ix[:]).then_inc(T.sem["lix"], 16)
+    ev["ix"] = ("lix", 128)
+    did(g.sync.dma_start(T.wmt[:], T.wm[:]), "lwm", "wm", 16)
+    did(g.sync.dma_start(T.dlt[:], T.dl[:]), "ldl", "dl", 16)
+    did(g.sync.dma_start(T.xt[:, 0:1024], T.x[:, 0:1024]), "lx0", "x0", 16)
+    after("y", "wm")
+    did(g.sync.dma_start(T.xt[:, 1024:2048], T.x[:, 1024:2048]), "lx1", "x1", 16)
+
+    did(g.iota(T.pi[:], [[0, 2]], 0, 1), "sg", "pi")
+    did(g.iota(T.pk[:], [[16, 16]], 0, 1), "sg", "pk")
+    did(g.iota(T.vals[:], [[1, NEW]], 0, 0, allow_small_or_imprecise_dtypes=True), "sg", "vals")
+    did(v.memset(T.row[:], LOW), "sv", "row")
+    after("v", "pi")
+    did(v.tensor_scalar(T.si[:], T.pi[:], 4, 1, A.logical_shift_right, A.bitwise_and), "sv", "si")
+    did(v.tensor_scalar(T.hi[:], T.pi[:], 4, None, A.logical_shift_right), "sv", "hi")
+    after("v", "si")
+    for t in range(R):
+        did(v.tensor_scalar(T.pos[:, 2 * t:2 * t + 2], T.si[:], -16, 32 + (SEG if t == 2 else 0), A.mult, A.add), "sv", "pos")
+    did(v.tensor_copy(T.odd[:], T.si[:]), "sv", "odd")
+    did(v.tensor_scalar(T.even[:], T.si[:], -1, 1, A.mult, A.add), "sv", "even")
+    after("v", "hi")
+    did(v.tensor_scalar(T.hf[:], T.hi[:], -16, -SH, A.mult, A.add), "sv", "hf")
+    after("v", "hf", "pk")
+    did(v.tensor_scalar(T.ident[:], T.pk[:], T.hf[:, 0:1], None, A.add), "sv", "ident")
+
+    after("v", "ix", "pos")
+    for t in range(R):
+        did(v.tensor_scalar(T.off[:, 4 * t:4 * t + 4], T.lst[:, 4 * t:4 * t + 4], T.pos[:, 2 * t:2 * t + 1], None, A.add), "sv", "off")
+    after("v", "off", "row", "vals")
+    did(v.tensor_copy(T.row[:, 0:SEG].indirect(T.off[:, 0:4]), T.vals[:, 0:CH]), "sv", "scat1")
+    after("v", "wm")
+    did(v.quantize_mx(win[:, 0:SH], scl[:, 0:SH], T.wmt[:]), "sv", "base")
+    after("v", "dl")
+    did(v.quantize_mx(win[:, SH:HELD], scl[:, SH:HELD], T.dlt[:]), "sv", "delta")
+    ev["codes%d" % r] = ev["scales%d" % r] = ev["delta"]
+    did(v.tensor_copy(T.row[:, SEG:R * SEG].indirect(T.off[:, 4:12]), T.vals[:, CH:NEW]), "sv", "scat2")
+
+    after("v", "scat1", "scat2")
+    did(v.transpose(T.tr[:], T.row[:]), "sv", "tr")
+    after("v", "tr", "odd", "even")
+    did(v.tensor_scalar(T.pa[:], T.tr[:, 0:R * SEG:16], T.even[:, 0:1], None, A.mult), "sv", "pa")
+    did(v.tensor_scalar(T.pb[:], T.tr[:, 0:R * SEG:16], T.odd[:, 0:1], None, A.mult), "sv", "pb")
+    after("v", "pa", "pb")
+    did(v.tensor_tensor(T.gg[:], T.pa[:, 2:54], T.pb[:, 1:53], A.add), "sv", "gg")
+    after("v", "gg", "ident")
+    did(v.tensor_tensor(T.mt[:, 0:16], T.gg[:, 0:16], T.ident[:], A.max), "sv", "m1")
+    after("v", "m1")
+    did(v.tensor_tensor(T.mt[:, 16:32], T.gg[:, 18:34], T.mt[:, 0:16], A.max), "sv", "m2")
+    after("v", "m2")
+    did(v.tensor_tensor(T.mt[:, 32:48], T.gg[:, 36:52], T.mt[:, 16:32], A.max), "sv", "m3")
+    after("v", "m3")
+    did(v.tensor_scalar(tab[:], T.mt[:], SH, None, A.add), "sv", "tab")
+    for t in (1, 2, 3):
+        ev["tab%d_%d" % (r, t)] = ev["tab"]
+
+    send_scales(r, [near])
+    send_codes(r, [near])
+    send_scales(r, [far1])
+    after("y", "tab")
+    did(g.sync.dma_start(T.tdram[:], tab[0:16, 16:48]), "tdr", "tdram", 16)
+    after("g", "tab")
+    send(tab[:], tab[:], "at%d" % r, [near])
+    send(tab[:, 0:16], tab[:, 0:16], "at%d" % r, [far1, far2])
+    send_codes(r, [far1])
+    after("g", "tdram")
+    send(T.tdram[:], T["ld%d" % r][:], "ad%d" % r, [far1, far2])
+    send_scales(far1, [near])
+    send_codes(far1, [near])
+
+    def qx(h):
+        after("v", "x%d" % h)
+        did(v.quantize_mx(T.xq[:, 256 * h:256 * h + 256], T.xsc[:, 256 * h:256 * h + 256], T.xt[:, 1024 * h:1024 * h + 1024]), "sv", "xq%d" % h)
+
+    def pick(q, t):
+        h, c = q // 2, SH * (q % 2)
+        o = T["tab%d" % q][:, 16 * t - 16:16 * t]
+        after("v", "codes%d" % q, "tab%d_%d" % (q, t))
+        did(v.tensor_copy(T["wc%d%d" % (h, t)][:, c:c + SH].bitcast(dt.uint32), T["win%d" % q][:].bitcast(dt.uint32).indirect(o)),
+            "sv", "pc%d%d" % (q, t))
+        after("s", "scales%d" % q, "tab%d_%d" % (q, t))
+        did(g.scalar.activation(T["ws%d%d" % (h, t)][:, c:c + SH], T["scl%d" % q][:].indirect(o), COPY), "ss", "pq%d%d" % (q, t))
+
+    def product(t, ranks, bank, frees=None):
+        h = ranks[0] // 2
+        after("t", "xq%d" % (t // 2))
+        if frees:
+            after("t", frees)
+        for q in ranks:
+            after("t", *(("codes%d" % q, "scales%d" % q) if t == 0 else ("pc%d%d" % (q, t), "pq%d%d" % (q, t))))
+        n = SH * len(ranks)
+        c = SH * (ranks[0] % 2)
+        if t == 0:
+            rhs, rs = T["win%d" % ranks[0]][:, 0:SH], T["scl%d" % ranks[0]][:, 0:SH]
+        else:
+            rhs, rs = T["wc%d%d" % (h, t)][:, c:c + n], T["ws%d%d" % (h, t)][:, c:c + n]
+        x0 = 128 * t
+        did(g.tensor.matmul_mx(T["ps%d" % bank][:, 0:n], T.xq[:, x0:x0 + 128], T.xsc[:, x0:x0 + 128], rhs, rs, True, True),
+            "st", "p%d_%d" % (t, ranks[0]))
+
+    def evac(qn, t, ranks, bank):
+        h, c, n = ranks[0] // 2, SH * (ranks[0] % 2), SH * len(ranks)
+        after(qn, "p%d_%d" % (t, ranks[0]))
+        out, src = T["y%d%d" % (h, t)][:, c:c + n], T["ps%d" % bank][:, 0:n]
+        if qn == "v":
+            did(v.tensor_copy(out, src), "sv", "e%d_%d" % (t, ranks[0]))
+        else:
+            did(g.scalar.activation(out, src, COPY), "ss", "e%d_%d" % (t, ranks[0]))
+
+    def store(t, h, *evs):
+        after("y", *evs)
+        k = SH * (t * N + 2 * h)
+        did(g.sync.dma_start(T.y[:, k:k + 512], T["y%d%d" % (h, t)][:]), "ysem", "y", 16)
+
+    def repeat(q):
+        after("y", "ld%d" % q)
+        for k in range(8):
+            g.sync.dma_start(T["tab%d" % q][16 * k:16 * k + 16, 16:48], T["ld%d" % q][:]).then_inc(T.sem["tl%d" % q], 16)
+
+    home, away = [2 * hh, 2 * hh + 1], [2 * fh, 2 * fh + 1]
+    h0, a0 = home[0], away[0]
+    qx(0)
+    product(0, [r], 0)
+    for t in (1, 2, 3):
+        pick(r, t)
+    evac("s", 0, [r], 0)
+    qx(1)
+    product(0, [near], 1)
+    evac("v", 0, [near], 1)
+    store(0, hh, "e0_%d" % r, "e0_%d" % near)
+    pick(near, 1)
+    product(1, home, 2)
+    pick(near, 2)
+    product(2, home, 3)
+    evac("s", 1, home, 2)
+    store(1, hh, "e1_%d" % h0)
+    repeat(far1)
+    repeat(far2)
+    pick(near, 3)
+    product(3, home, 4)
+    evac("v", 2, home, 3)
+    store(2, hh, "e2_%d" % h0)
+    product(0, [far1], 5)
+    product(0, [far2], 6)
+    pick(far1, 1)
+    evac("s", 3, home, 4)
+    store(3, hh, "e3_%d" % h0)
+    evac("s", 0, [far1], 5)
+    pick(far2, 1)
+    evac("s", 0, [far2], 6)
+    store(0, fh, "e0_%d" % far1, "e0_%d" % far2)
+    product(1, away, 7)
+    pick(far1, 2)
+    pick(far2, 2)
+    product(2, away, 0, frees="e0_%d" % r)
+    evac("v", 1, away, 7)
+    store(1, fh, "e1_%d" % a0)
+    pick(far1, 3)
+    product(3, [far1], 1, frees="e0_%d" % near)
+    pick(far2, 3)
+    product(3, [far2], 2, frees="e1_%d" % h0)
+    evac("v", 2, away, 0)
+    store(2, fh, "e2_%d" % a0)
+    evac("v", 3, [far1], 1)
+    evac("s", 3, [far2], 2)
+    store(3, fh, "e3_%d" % far1, "e3_%d" % far2)
+
+    g.wait_ge(T.sem["ls"], nls[0])
+    after("y", "y")

@@ -24,26 +24,26 @@ SCRATCH = {
     "hi": ("sbuf", [128, 2], "int32"),
     "odd": ("sbuf", [128, 2], "float32"),
     "even": ("sbuf", [128, 2], "float32"),
-    "pos": ("sbuf", [128, 6], "float32"),
+    "pos": ("sbuf", [128, 2], "float32"),
     "hf": ("sbuf", [128, 2], "float32"),
     "ident": ("sbuf", [128, 16], "float32"),
     "pa": ("sbuf", [128, 54], "float32"),
     "pb": ("sbuf", [128, 54], "float32"),
     "gg": ("sbuf", [128, 52], "float32"),
+    "nn": ("sbuf", [128, 16], "float32"),
     "mt": ("sbuf", [128, 48], "float32"),
     "tdram": ("dram", [128, 4], "uint16"),
 }
 for _q in range(N):
     SCRATCH["win%d" % _q] = ("sbuf", [128, HELD], "float8_e4m3fn_x4")
     SCRATCH["scl%d" % _q] = ("sbuf", [128, HELD], "uint8")
+    SCRATCH["wc%d" % _q] = ("sbuf", [128, R * SH], "float8_e4m3fn_x4")
+    SCRATCH["ws%d" % _q] = ("sbuf", [128, R * SH], "uint8")
     SCRATCH["tab%d" % _q] = ("sbuf", [128, 48], "uint16")
     SCRATCH["ld%d" % _q] = ("dram", [128, 4], "uint16")
 for _h in range(2):
     for _t in range(R + 1):
         SCRATCH["y%d%d" % (_h, _t)] = ("sbuf", [128, 512], "float32")
-        if _t:
-            SCRATCH["wc%d%d" % (_h, _t)] = ("sbuf", [128, 512], "float8_e4m3fn_x4")
-            SCRATCH["ws%d%d" % (_h, _t)] = ("sbuf", [128, 512], "uint8")
 for _b in range(8):
     SCRATCH["ps%d" % _b] = ("psum", [128, 512], "float32")
 
@@ -133,8 +133,7 @@ def rank_program(g, core, T, topo):
     did(v.tensor_scalar(T.si[:], T.pi[:], 4, 1, A.logical_shift_right, A.bitwise_and), "sv", "si")
     did(v.tensor_scalar(T.hi[:], T.pi[:], 4, None, A.logical_shift_right), "sv", "hi")
     after("v", "si")
-    for t in range(R):
-        did(v.tensor_scalar(T.pos[:, 2 * t:2 * t + 2], T.si[:], -16, 32 + (SEG if t == 2 else 0), A.mult, A.add), "sv", "pos")
+    did(v.tensor_scalar(T.pos[:], T.si[:], -16, 32, A.mult, A.add), "sv", "pos")
     did(v.tensor_copy(T.odd[:], T.si[:]), "sv", "odd")
     did(v.tensor_scalar(T.even[:], T.si[:], -1, 1, A.mult, A.add), "sv", "even")
     after("v", "hi")
@@ -142,91 +141,48 @@ def rank_program(g, core, T, topo):
     after("v", "hf", "pk")
     did(v.tensor_scalar(T.ident[:], T.pk[:], T.hf[:, 0:1], None, A.add), "sv", "ident")
 
-    after("v", "ix", "pos")
-    for t in range(R):
-        did(v.tensor_scalar(T.off[:, 4 * t:4 * t + 4], T.lst[:, 4 * t:4 * t + 4], T.pos[:, 2 * t:2 * t + 1], None, A.add), "sv", "off")
-    after("v", "off", "row", "vals")
-    did(v.tensor_copy(T.row[:, 0:SEG].indirect(T.off[:, 0:4]), T.vals[:, 0:CH]), "sv", "scat1")
-    after("v", "wm")
-    did(v.quantize_mx(win[:, 0:SH], scl[:, 0:SH], T.wmt[:]), "sv", "base")
-    after("v", "dl")
-    did(v.quantize_mx(win[:, SH:HELD], scl[:, SH:HELD], T.dlt[:]), "sv", "delta")
-    ev["codes%d" % r] = ev["scales%d" % r] = ev["delta"]
-    did(v.tensor_copy(T.row[:, SEG:R * SEG].indirect(T.off[:, 4:12]), T.vals[:, CH:NEW]), "sv", "scat2")
-
-    after("v", "scat1", "scat2")
-    did(v.transpose(T.tr[:], T.row[:]), "sv", "tr")
-    after("v", "tr", "odd", "even")
-    did(v.tensor_scalar(T.pa[:], T.tr[:, 0:R * SEG:16], T.even[:, 0:1], None, A.mult), "sv", "pa")
-    did(v.tensor_scalar(T.pb[:], T.tr[:, 0:R * SEG:16], T.odd[:, 0:1], None, A.mult), "sv", "pb")
-    after("v", "pa", "pb")
-    did(v.tensor_tensor(T.gg[:], T.pa[:, 2:54], T.pb[:, 1:53], A.add), "sv", "gg")
-    after("v", "gg", "ident")
-    did(v.tensor_tensor(T.mt[:, 0:16], T.gg[:, 0:16], T.ident[:], A.max), "sv", "m1")
-    after("v", "m1")
-    did(v.tensor_tensor(T.mt[:, 16:32], T.gg[:, 18:34], T.mt[:, 0:16], A.max), "sv", "m2")
-    after("v", "m2")
-    did(v.tensor_tensor(T.mt[:, 32:48], T.gg[:, 36:52], T.mt[:, 16:32], A.max), "sv", "m3")
-    after("v", "m3")
-    did(v.tensor_scalar(tab[:], T.mt[:], SH, None, A.add), "sv", "tab")
-    for t in (1, 2, 3):
-        ev["tab%d_%d" % (r, t)] = ev["tab"]
-
-    send_scales(r, [near])
-    send_codes(r, [near])
-    send_scales(r, [far1])
-    after("y", "tab")
-    did(g.sync.dma_start(T.tdram[:], tab[0:16, 16:48]), "tdr", "tdram", 16)
-    after("g", "tab")
-    send(tab[:], tab[:], "at%d" % r, [near])
-    send(tab[:, 0:16], tab[:, 0:16], "at%d" % r, [far1, far2])
-    send_codes(r, [far1])
-    after("g", "tdram")
-    send(T.tdram[:], T["ld%d" % r][:], "ad%d" % r, [far1, far2])
-    send_scales(far1, [near])
-    send_codes(far1, [near])
-
     def qx(h):
         after("v", "x%d" % h)
         did(v.quantize_mx(T.xq[:, 256 * h:256 * h + 256], T.xsc[:, 256 * h:256 * h + 256], T.xt[:, 1024 * h:1024 * h + 1024]), "sv", "xq%d" % h)
 
-    def pick(q, t):
-        h, c = q // 2, SH * (q % 2)
-        o = T["tab%d" % q][:, 16 * t - 16:16 * t]
-        after("v", "codes%d" % q, "tab%d_%d" % (q, t))
-        did(v.tensor_copy(T["wc%d%d" % (h, t)][:, c:c + SH].bitcast(dt.uint32), T["win%d" % q][:].bitcast(dt.uint32).indirect(o)),
-            "sv", "pc%d%d" % (q, t))
-        after("s", "scales%d" % q, "tab%d_%d" % (q, t))
-        did(g.scalar.activation(T["ws%d%d" % (h, t)][:, c:c + SH], T["scl%d" % q][:].indirect(o), COPY), "ss", "pq%d%d" % (q, t))
+    def pick(q, t0, t1):
+        a, b = SH * (t0 - 1), SH * t1
+        o = T["tab%d" % q][:, 16 * (t0 - 1):16 * t1]
+        after("v", "codes%d" % q, "tab%d_%d" % (q, t1))
+        did(v.tensor_copy(T["wc%d" % q][:, a:b].bitcast(dt.uint32), T["win%d" % q][:].bitcast(dt.uint32).indirect(o)), "sv", "pc")
+        after("s", "scales%d" % q, "tab%d_%d" % (q, t1))
+        did(g.scalar.activation(T["ws%d" % q][:, a:b], T["scl%d" % q][:].indirect(o), COPY), "ss", "pq")
+        for t in range(t0, t1 + 1):
+            ev["pc%d%d" % (q, t)], ev["pq%d%d" % (q, t)] = ev["pc"], ev["pq"]
 
-    def product(t, ranks, bank, frees=None):
-        h = ranks[0] // 2
+    bank = {}
+    last = {}
+
+    def product(t, q):
+        b = len(bank) % 8
         after("t", "xq%d" % (t // 2))
-        if frees:
-            after("t", frees)
-        for q in ranks:
-            after("t", *(("codes%d" % q, "scales%d" % q) if t == 0 else ("pc%d%d" % (q, t), "pq%d%d" % (q, t))))
-        n = SH * len(ranks)
-        c = SH * (ranks[0] % 2)
-        if t == 0:
-            rhs, rs = T["win%d" % ranks[0]][:, 0:SH], T["scl%d" % ranks[0]][:, 0:SH]
-        else:
-            rhs, rs = T["wc%d%d" % (h, t)][:, c:c + n], T["ws%d%d" % (h, t)][:, c:c + n]
+        if b in last:
+            after("t", last[b])
+        after("t", *(("codes%d" % q, "scales%d" % q) if t == 0 else ("pc%d%d" % (q, t), "pq%d%d" % (q, t))))
+        w, sc = ("win%d", "scl%d") if t == 0 else ("wc%d", "ws%d")
+        c = SH * max(t - 1, 0)
         x0 = 128 * t
-        did(g.tensor.matmul_mx(T["ps%d" % bank][:, 0:n], T.xq[:, x0:x0 + 128], T.xsc[:, x0:x0 + 128], rhs, rs, True, True),
-            "st", "p%d_%d" % (t, ranks[0]))
+        did(g.tensor.matmul_mx(T["ps%d" % b][:, 0:SH], T.xq[:, x0:x0 + 128], T.xsc[:, x0:x0 + 128],
+                               T[w % q][:, c:c + SH], T[sc % q][:, c:c + SH], True, True), "st", "p%d_%d" % (t, q))
+        bank[(t, q)] = b
+        last[b] = "e%d_%d" % (t, q)
 
-    def evac(qn, t, ranks, bank):
-        h, c, n = ranks[0] // 2, SH * (ranks[0] % 2), SH * len(ranks)
-        after(qn, "p%d_%d" % (t, ranks[0]))
-        out, src = T["y%d%d" % (h, t)][:, c:c + n], T["ps%d" % bank][:, 0:n]
+    def evac(qn, t, q):
+        c = SH * (q % 2)
+        after(qn, "p%d_%d" % (t, q))
+        out, src = T["y%d%d" % (q // 2, t)][:, c:c + SH], T["ps%d" % bank[(t, q)]][:, 0:SH]
         if qn == "v":
-            did(v.tensor_copy(out, src), "sv", "e%d_%d" % (t, ranks[0]))
+            did(v.tensor_copy(out, src), "sv", "e%d_%d" % (t, q))
         else:
-            did(g.scalar.activation(out, src, COPY), "ss", "e%d_%d" % (t, ranks[0]))
+            did(g.scalar.activation(out, src, COPY), "ss", "e%d_%d" % (t, q))
 
-    def store(t, h, *evs):
-        after("y", *evs)
+    def store(t, h):
+        after("y", "e%d_%d" % (t, 2 * h), "e%d_%d" % (t, 2 * h + 1))
         k = SH * (t * N + 2 * h)
         did(g.sync.dma_start(T.y[:, k:k + 512], T["y%d%d" % (h, t)][:]), "ysem", "y", 16)
 
@@ -235,53 +191,104 @@ def rank_program(g, core, T, topo):
         for k in range(8):
             g.sync.dma_start(T["tab%d" % q][16 * k:16 * k + 16, 16:48], T["ld%d" % q][:]).then_inc(T.sem["tl%d" % q], 16)
 
-    home, away = [2 * hh, 2 * hh + 1], [2 * fh, 2 * fh + 1]
-    h0, a0 = home[0], away[0]
+    after("v", "ix", "pos")
+    did(v.tensor_scalar(T.off[:], T.lst[:], T.pos[:, 0:1], None, A.add), "sv", "off")
+
+    def scatter(t):
+        after("v", "off", "row", "vals")
+        did(v.tensor_copy(T.row[:, SEG * t:SEG * t + SEG].indirect(T.off[:, 4 * t:4 * t + 4]), T.vals[:, CH * t:CH * t + CH]), "sv", "scat")
+
+    scatter(0)
+    after("v", "wm")
+    did(v.quantize_mx(win[:, 0:SH], scl[:, 0:SH], T.wmt[:]), "sv", "base")
+    after("v", "dl")
+    did(v.quantize_mx(win[:, SH:HELD], scl[:, SH:HELD], T.dlt[:]), "sv", "delta")
+    ev["codes%d" % r] = ev["scales%d" % r] = ev["delta"]
+    scatter(1)
+    scatter(2)
+
+    after("v", "scat")
+    did(v.transpose(T.tr[:], T.row[:]), "sv", "tr")
     qx(0)
-    product(0, [r], 0)
+    product(0, r)
+    evac("s", 0, r)
+    after("v", "tr", "odd", "even")
+    did(v.tensor_scalar(T.pa[:], T.tr[:, 0:R * SEG:16], T.even[:, 0:1], None, A.mult), "sv", "pa")
+    did(v.tensor_scalar(T.pb[:], T.tr[:, 0:R * SEG:16], T.odd[:, 0:1], None, A.mult), "sv", "pb")
+    after("v", "pa", "pb")
+    did(v.tensor_tensor(T.gg[:], T.pa[:, 2:54], T.pb[:, 1:53], A.add), "sv", "gg")
+    after("v", "gg", "ident")
+    did(v.tensor_tensor(T.mt[:, 0:16], T.gg[:, 0:16], T.ident[:], A.max), "sv", "m1")
+    did(v.tensor_tensor(T.nn[:], T.gg[:, 18:34], T.gg[:, 36:52], A.max), "sv", "nn")
+    after("v", "m1", "nn")
+    did(v.tensor_tensor(T.mt[:, 16:32], T.gg[:, 18:34], T.mt[:, 0:16], A.max), "sv", "m2")
+    did(v.tensor_tensor(T.mt[:, 32:48], T.nn[:], T.mt[:, 0:16], A.max), "sv", "m3")
+    after("v", "m2", "m3")
+    did(v.tensor_scalar(tab[:], T.mt[:], SH, None, A.add), "sv", "tab")
     for t in (1, 2, 3):
-        pick(r, t)
-    evac("s", 0, [r], 0)
+        ev["tab%d_%d" % (r, t)] = ev["tab"]
+
+    send_scales(r, [far1])
+    send_scales(r, [near])
+    send_codes(r, [near])
+    after("y", "tab")
+    did(g.sync.dma_start(T.tdram[:], tab[0:16, 16:48]), "tdr", "tdram", 16)
+    after("g", "tab")
+    send(tab[:], tab[:], "at%d" % r, [near])
+    send_codes(r, [far1])
+    send(tab[:, 0:16], tab[:, 0:16], "at%d" % r, [far1, far2])
+    after("g", "tdram")
+    send(T.tdram[:], T["ld%d" % r][:], "ad%d" % r, [far1, far2])
+    send_scales(far1, [near])
+    send_codes(far1, [near])
+
     qx(1)
-    product(0, [near], 1)
-    evac("v", 0, [near], 1)
-    store(0, hh, "e0_%d" % r, "e0_%d" % near)
-    pick(near, 1)
-    product(1, home, 2)
-    pick(near, 2)
-    product(2, home, 3)
-    evac("s", 1, home, 2)
-    store(1, hh, "e1_%d" % h0)
+    pick(r, 1, 3)
+    product(0, near)
+    evac("v", 0, near)
+    store(0, hh)
+    for t in (1, 2, 3):
+        product(t, r)
+    pick(near, 1, 2)
+    pick(near, 3, 3)
+    evac("s", 1, r)
+    evac("v", 2, r)
+    for t in (1, 2, 3):
+        product(t, near)
+    evac("s", 3, r)
     repeat(far1)
     repeat(far2)
-    pick(near, 3)
-    product(3, home, 4)
-    evac("v", 2, home, 3)
-    store(2, hh, "e2_%d" % h0)
-    product(0, [far1], 5)
-    product(0, [far2], 6)
-    pick(far1, 1)
-    evac("s", 3, home, 4)
-    store(3, hh, "e3_%d" % h0)
-    evac("s", 0, [far1], 5)
-    pick(far2, 1)
-    evac("s", 0, [far2], 6)
-    store(0, fh, "e0_%d" % far1, "e0_%d" % far2)
-    product(1, away, 7)
-    pick(far1, 2)
-    pick(far2, 2)
-    product(2, away, 0, frees="e0_%d" % r)
-    evac("v", 1, away, 7)
-    store(1, fh, "e1_%d" % a0)
-    pick(far1, 3)
-    product(3, [far1], 1, frees="e0_%d" % near)
-    pick(far2, 3)
-    product(3, [far2], 2, frees="e1_%d" % h0)
-    evac("v", 2, away, 0)
-    store(2, fh, "e2_%d" % a0)
-    evac("v", 3, [far1], 1)
-    evac("s", 3, [far2], 2)
-    store(3, fh, "e3_%d" % far1, "e3_%d" % far2)
+    pick(far1, 1, 1)
+    evac("s", 1, near)
+    evac("v", 2, near)
+    store(1, hh)
+    store(2, hh)
+    product(0, far1)
+    product(0, far2)
+    evac("s", 3, near)
+    store(3, hh)
+    pick(far2, 1, 1)
+    evac("s", 0, far1)
+    evac("s", 0, far2)
+    store(0, fh)
+    product(1, far1)
+    product(1, far2)
+    pick(far1, 2, 3)
+    evac("v", 1, far1)
+    evac("s", 1, far2)
+    store(1, fh)
+    product(2, far1)
+    product(3, far1)
+    pick(far2, 2, 2)
+    pick(far2, 3, 3)
+    product(2, far2)
+    evac("v", 2, far1)
+    product(3, far2)
+    evac("s", 2, far2)
+    store(2, fh)
+    evac("v", 3, far1)
+    evac("s", 3, far2)
+    store(3, fh)
 
     g.wait_ge(T.sem["ls"], nls[0])
     after("y", "y")

@@ -19,19 +19,17 @@ SCRATCH = {
     "row": ("sbuf", [128, R * SEG], "bfloat16"),
     "tr": ("sbuf", [128, R * SEG], "bfloat16"),
     "pi": ("sbuf", [128, 2], "int32"),
-    "pk": ("sbuf", [128, 16], "int32"),
+    "up": ("sbuf", [128, SEG], "float32"),
     "si": ("sbuf", [128, 2], "int32"),
-    "hi": ("sbuf", [128, 2], "int32"),
+    "sh": ("sbuf", [128, 2], "float32"),
     "odd": ("sbuf", [128, 2], "float32"),
     "even": ("sbuf", [128, 2], "float32"),
     "pos": ("sbuf", [128, 2], "float32"),
-    "hf": ("sbuf", [128, 2], "float32"),
-    "ident": ("sbuf", [128, 16], "float32"),
     "pa": ("sbuf", [128, 54], "float32"),
     "pb": ("sbuf", [128, 54], "float32"),
     "gg": ("sbuf", [128, 52], "float32"),
     "nn": ("sbuf", [128, 16], "float32"),
-    "mt": ("sbuf", [128, 48], "float32"),
+    "mt": ("sbuf", [128, 32], "float32"),
     "tdram": ("dram", [128, 4], "uint16"),
 }
 for _q in range(N):
@@ -126,20 +124,18 @@ def rank_program(g, core, T, topo):
     did(g.sync.dma_start(T.xt[:, 1024:2048], T.x[:, 1024:2048]), "lx1", "x1", 16)
 
     did(g.iota(T.pi[:], [[0, 2]], 0, 1), "sg", "pi")
-    did(g.iota(T.pk[:], [[16, 16]], 0, 1), "sg", "pk")
+    did(g.iota(T.up[:], [[1, SEG]], -SEG, 0, allow_small_or_imprecise_dtypes=True), "sg", "up")
     did(g.iota(T.vals[:], [[1, NEW]], 0, 0, allow_small_or_imprecise_dtypes=True), "sg", "vals")
-    did(v.memset(T.row[:], LOW), "sv", "row")
     after("v", "pi")
     did(v.tensor_scalar(T.si[:], T.pi[:], 4, 1, A.logical_shift_right, A.bitwise_and), "sv", "si")
-    did(v.tensor_scalar(T.hi[:], T.pi[:], 4, None, A.logical_shift_right), "sv", "hi")
+    did(v.memset(T.row[:, SEG:R * SEG], LOW), "sv", "low")
     after("v", "si")
+    did(v.tensor_scalar(T.sh[:], T.si[:], 16, None, A.mult), "sv", "sh")
     did(v.tensor_scalar(T.pos[:], T.si[:], -16, 32, A.mult, A.add), "sv", "pos")
     did(v.tensor_copy(T.odd[:], T.si[:]), "sv", "odd")
     did(v.tensor_scalar(T.even[:], T.si[:], -1, 1, A.mult, A.add), "sv", "even")
-    after("v", "hi")
-    did(v.tensor_scalar(T.hf[:], T.hi[:], -16, -SH, A.mult, A.add), "sv", "hf")
-    after("v", "hf", "pk")
-    did(v.tensor_scalar(T.ident[:], T.pk[:], T.hf[:, 0:1], None, A.add), "sv", "ident")
+    after("v", "sh", "up")
+    did(v.tensor_scalar(T.row[:, 0:SEG], T.up[:], T.sh[:, 0:1], None, A.add), "sv", "row")
 
     def qx(h):
         after("v", "x%d" % h)
@@ -193,19 +189,14 @@ def rank_program(g, core, T, topo):
 
     after("v", "ix", "pos")
     did(v.tensor_scalar(T.off[:], T.lst[:], T.pos[:, 0:1], None, A.add), "sv", "off")
-
-    def scatter(t):
-        after("v", "off", "row", "vals")
+    after("v", "off", "row", "low", "vals")
+    for t in range(R):
         did(v.tensor_copy(T.row[:, SEG * t:SEG * t + SEG].indirect(T.off[:, 4 * t:4 * t + 4]), T.vals[:, CH * t:CH * t + CH]), "sv", "scat")
-
-    scatter(0)
     after("v", "wm")
     did(v.quantize_mx(win[:, 0:SH], scl[:, 0:SH], T.wmt[:]), "sv", "base")
     after("v", "dl")
     did(v.quantize_mx(win[:, SH:HELD], scl[:, SH:HELD], T.dlt[:]), "sv", "delta")
     ev["codes%d" % r] = ev["scales%d" % r] = ev["delta"]
-    scatter(1)
-    scatter(2)
 
     after("v", "scat")
     did(v.transpose(T.tr[:], T.row[:]), "sv", "tr")
@@ -217,14 +208,14 @@ def rank_program(g, core, T, topo):
     did(v.tensor_scalar(T.pb[:], T.tr[:, 0:R * SEG:16], T.odd[:, 0:1], None, A.mult), "sv", "pb")
     after("v", "pa", "pb")
     did(v.tensor_tensor(T.gg[:], T.pa[:, 2:54], T.pb[:, 1:53], A.add), "sv", "gg")
-    after("v", "gg", "ident")
-    did(v.tensor_tensor(T.mt[:, 0:16], T.gg[:, 0:16], T.ident[:], A.max), "sv", "m1")
+    after("v", "gg")
+    did(v.tensor_tensor(T.mt[:, 0:16], T.gg[:, 0:16], T.gg[:, 18:34], A.max), "sv", "m2")
     did(v.tensor_tensor(T.nn[:], T.gg[:, 18:34], T.gg[:, 36:52], A.max), "sv", "nn")
-    after("v", "m1", "nn")
-    did(v.tensor_tensor(T.mt[:, 16:32], T.gg[:, 18:34], T.mt[:, 0:16], A.max), "sv", "m2")
-    did(v.tensor_tensor(T.mt[:, 32:48], T.nn[:], T.mt[:, 0:16], A.max), "sv", "m3")
-    after("v", "m2", "m3")
-    did(v.tensor_scalar(tab[:], T.mt[:], SH, None, A.add), "sv", "tab")
+    did(v.tensor_scalar(tab[:, 0:16], T.gg[:, 0:16], SH, None, A.add), "sv", "tab1")
+    after("v", "nn")
+    did(v.tensor_tensor(T.mt[:, 16:32], T.nn[:], T.gg[:, 0:16], A.max), "sv", "m3")
+    after("v", "m3")
+    did(v.tensor_scalar(tab[:, 16:48], T.mt[:], SH, None, A.add), "sv", "tab")
     for t in (1, 2, 3):
         ev["tab%d_%d" % (r, t)] = ev["tab"]
 
@@ -251,7 +242,7 @@ def rank_program(g, core, T, topo):
         product(t, r)
     pick(near, 1, 2)
     pick(near, 3, 3)
-    evac("s", 1, r)
+    evac("v", 1, r)
     evac("v", 2, r)
     for t in (1, 2, 3):
         product(t, near)
@@ -269,17 +260,17 @@ def rank_program(g, core, T, topo):
     store(3, hh)
     pick(far2, 1, 1)
     evac("s", 0, far1)
-    evac("s", 0, far2)
+    evac("v", 0, far2)
     store(0, fh)
     product(1, far1)
     product(1, far2)
     pick(far1, 2, 3)
+    pick(far2, 2, 2)
     evac("v", 1, far1)
     evac("s", 1, far2)
     store(1, fh)
     product(2, far1)
     product(3, far1)
-    pick(far2, 2, 2)
     pick(far2, 3, 3)
     product(2, far2)
     evac("v", 2, far1)

from concourse.bass import DstId, RemoteDMATransfer
from concourse.mybir import dt, AluOpType, ActivationFunctionType

N, SH, CH, R = 4, 256, 64, 3
NEW = R * CH
HELD = SH + NEW
SEG = SH + 32
LOW = -8192.0

SCRATCH = {
    "wmt": ("sbuf", [128, 4 * SH], "bfloat16"),
    "dlt": ("sbuf", [128, 4 * NEW], "bfloat16"),
    "xt": ("sbuf", [128, 512 * (R + 1)], "bfloat16"),
    "xq": ("sbuf", [128, 512], "float8_e4m3fn_x4"),
    "xsc": ("sbuf", [128, 512], "uint8"),
    "lst": ("sbuf", [128, 12], "int32"),
    "off": ("sbuf", [128, 12], "uint16"),
    "vals": ("sbuf", [128, NEW], "bfloat16"),
    "row": ("sbuf", [128, R * SEG], "bfloat16"),
    "tr": ("sbuf", [128, R * SEG], "bfloat16"),
    "pi": ("sbuf", [128, 2], "int32"),
    "up": ("sbuf", [128, SEG], "float32"),
    "si": ("sbuf", [128, 2], "int32"),
    "sh": ("sbuf", [128, 2], "float32"),
    "odd": ("sbuf", [128, 2], "float32"),
    "even": ("sbuf", [128, 2], "float32"),
    "pos": ("sbuf", [128, 2], "float32"),
    "pa": ("sbuf", [128, 54], "float32"),
    "pb": ("sbuf", [128, 54], "float32"),
    "gg": ("sbuf", [128, 52], "float32"),
    "nn": ("sbuf", [128, 16], "float32"),
    "mt": ("sbuf", [128, 32], "float32"),
    "tdram": ("dram", [128, 4], "uint16"),
}
for _q in range(N):
    SCRATCH["win%d" % _q] = ("sbuf", [128, HELD], "float8_e4m3fn_x4")
    SCRATCH["scl%d" % _q] = ("sbuf", [128, HELD], "uint8")
    SCRATCH["wc%d" % _q] = ("sbuf", [128, R * SH], "float8_e4m3fn_x4")
    SCRATCH["ws%d" % _q] = ("sbuf", [128, R * SH], "uint8")
    SCRATCH["tab%d" % _q] = ("sbuf", [128, 48], "uint16")
    SCRATCH["ld%d" % _q] = ("dram", [128, 4], "uint16")
for _h in range(2):
    for _t in range(R + 1):
        SCRATCH["y%d%d" % (_h, _t)] = ("sbuf", [128, 512], "float32")
for _b in range(8):
    SCRATCH["ps%d" % _b] = ("psum", [128, 512], "float32")

SEMAPHORES = ["sv", "ss", "st", "sg", "lix", "lwm", "ldl", "lx0", "lx1", "tdr", "ysem", "ls"]
for _q in range(N):
    SEMAPHORES += ["ac%d" % _q, "as%d" % _q, "at%d" % _q, "ad%d" % _q, "tl%d" % _q]


def rank_program(g, core, T, topo):
    r = T.rank_of(core)
    if r is None:
        return
    A = AluOpType
    COPY = ActivationFunctionType.Copy
    queues = {"v": g.vector, "s": g.scalar, "t": g.tensor, "g": g, "y": g.sync}
    count = {}
    ev = {}
    seen = {}

    def after(qn, *names):
        for n in names:
            sem, val = ev[n]
            if seen.get((qn, sem), 0) < val:
                queues[qn].wait_ge(T.sem[sem], val)
                seen[(qn, sem)] = val

    def did(ins, sem, name, n=1):
        count[sem] = count.get(sem, 0) + n
        ins.then_inc(T.sem[sem], n)
        ev[name] = (sem, count[sem])

    mine = [q for q in range(N) if topo.die(T.cores[q]) == topo.die(core)]
    other = [q for q in range(N) if q not in mine]
    near = [q for q in mine if q != r][0]
    i = mine.index(r)
    far1, far2 = other[i], other[1 - i]
    peers = [near, far1, far2]
    hh, fh = r // 2, far1 // 2
    for q in peers:
        ev["codes%d" % q] = ("ac%d" % q, 16)
        ev["scales%d" % q] = ("as%d" % q, 16)
        ev["tab%d_1" % q] = ("at%d" % q, 16)
        for t in (2, 3):
            ev["tab%d_%d" % (q, t)] = ("at%d" % q, 16) if q == near else ("tl%d" % q, 128)
        ev["ld%d" % q] = ("ad%d" % q, 16)

    nls = [0]

    def send(src, dst, sem, dsts):
        ids = []
        for q in dsts:
            rid, pid, _ = topo.addr(T.cores[q])
            ids.append(DstId(rid=rid, pnc=pid))
        m = topo.mask(core, T.cores[dsts[0]])
        g.remote_dma_fused([RemoteDMATransfer(dst_ids=ids, dma_engine_mask=m, remote_sem=T.sem[sem], srcs=[src],
                                              dsts=[dst for _ in dsts])], local_sem=T.sem["ls"])
        nls[0] += len(topo.engines(core, T.cores[dsts[0]]))

    def send_codes(q, dsts):
        after("g", "codes%d" % q)
        w = T["win%d" % q][:].bitcast(dt.uint8)
        send(w, w, "ac%d" % q, dsts)

    def send_scales(q, dsts):
        after("g", "scales%d" % q)
        w = T["scl%d" % q][:]
        send(w, w, "as%d" % q, dsts)

    win, scl, tab = T["win%d" % r], T["scl%d" % r], T["tab%d" % r]
    v = g.vector

    for k in range(4):
        g.sync.dma_start(T.lst[16 * k:16 * k + 16, :], T.ix[:]).then_inc(T.sem["lix"], 16)
        g.scalar.dma_start(T.lst[64 + 16 * k:80 + 16 * k, :], T.ix[:]).then_inc(T.sem["lix"], 16)
    ev["ix"] = ("lix", 128)
    did(g.sync.dma_start(T.wmt[:], T.wm[:]), "lwm", "wm", 16)
    did(g.sync.dma_start(T.dlt[:], T.dl[:]), "ldl", "dl", 16)
    did(g.sync.dma_start(T.xt[:, 0:1024], T.x[:, 0:1024]), "lx0", "x0", 16)
    after("y", "wm")
    did(g.sync.dma_start(T.xt[:, 1024:2048], T.x[:, 1024:2048]), "lx1", "x1", 16)

    did(g.iota(T.pi[:], [[0, 2]], 0, 1), "sg", "pi")
    did(g.iota(T.up[:], [[1, SEG]], -SEG, 0, allow_small_or_imprecise_dtypes=True), "sg", "up")
    did(g.iota(T.vals[:], [[1, NEW]], 0, 0, allow_small_or_imprecise_dtypes=True), "sg", "vals")
    after("v", "pi")
    did(v.tensor_scalar(T.si[:], T.pi[:], 4, 1, A.logical_shift_right, A.bitwise_and), "sv", "si")
    did(v.memset(T.row[:, SEG:R * SEG], LOW), "sv", "low")
    after("v", "si")
    did(v.tensor_scalar(T.sh[:], T.si[:], 16, None, A.mult), "sv", "sh")
    did(v.tensor_scalar(T.pos[:], T.si[:], -16, 32, A.mult, A.add), "sv", "pos")
    did(v.tensor_copy(T.odd[:], T.si[:]), "sv", "odd")
    did(v.tensor_scalar(T.even[:], T.si[:], -1, 1, A.mult, A.add), "sv", "even")
    after("v", "sh", "up")
    did(v.tensor_scalar(T.row[:, 0:SEG], T.up[:], T.sh[:, 0:1], None, A.add), "sv", "row")

    def qx(h):
        after("v", "x%d" % h)
        did(v.quantize_mx(T.xq[:, 256 * h:256 * h + 256], T.xsc[:, 256 * h:256 * h + 256], T.xt[:, 1024 * h:1024 * h + 1024]), "sv", "xq%d" % h)

    def pick(q, t0, t1):
        a, b = SH * (t0 - 1), SH * t1
        o = T["tab%d" % q][:, 16 * (t0 - 1):16 * t1]
        after("v", "codes%d" % q, "tab%d_%d" % (q, t1))
        did(v.tensor_copy(T["wc%d" % q][:, a:b].bitcast(dt.uint32), T["win%d" % q][:].bitcast(dt.uint32).indirect(o)), "sv", "pc")
        after("s", "scales%d" % q, "tab%d_%d" % (q, t1))
        did(g.scalar.activation(T["ws%d" % q][:, a:b], T["scl%d" % q][:].indirect(o), COPY), "ss", "pq")
        for t in range(t0, t1 + 1):
            ev["pc%d%d" % (q, t)], ev["pq%d%d" % (q, t)] = ev["pc"], ev["pq"]

    bank = {}
    last = {}

    def product(t, q):
        b = len(bank) % 8
        after("t", "xq%d" % (t // 2))
        if b in last:
            after("t", last[b])
        after("t", *(("codes%d" % q, "scales%d" % q) if t == 0 else ("pc%d%d" % (q, t), "pq%d%d" % (q, t))))
        w, sc = ("win%d", "scl%d") if t == 0 else ("wc%d", "ws%d")
        c = SH * max(t - 1, 0)
        x0 = 128 * t
        did(g.tensor.matmul_mx(T["ps%d" % b][:, 0:SH], T.xq[:, x0:x0 + 128], T.xsc[:, x0:x0 + 128],
                               T[w % q][:, c:c + SH], T[sc % q][:, c:c + SH], True, True), "st", "p%d_%d" % (t, q))
        bank[(t, q)] = b
        last[b] = "e%d_%d" % (t, q)

    def evac(qn, t, q):
        c = SH * (q % 2)
        after(qn, "p%d_%d" % (t, q))
        out, src = T["y%d%d" % (q // 2, t)][:, c:c + SH], T["ps%d" % bank[(t, q)]][:, 0:SH]
        if qn == "v":
            did(v.tensor_copy(out, src), "sv", "e%d_%d" % (t, q))
        else:
            did(g.scalar.activation(out, src, COPY), "ss", "e%d_%d" % (t, q))

    def store(t, h):
        after("y", "e%d_%d" % (t, 2 * h), "e%d_%d" % (t, 2 * h + 1))
        k = SH * (t * N + 2 * h)
        did(g.sync.dma_start(T.y[:, k:k + 512], T["y%d%d" % (h, t)][:]), "ysem", "y", 16)

    def repeat(q):
        after("y", "ld%d" % q)
        for k in range(8):
            g.sync.dma_start(T["tab%d" % q][16 * k:16 * k + 16, 16:48], T["ld%d" % q][:]).then_inc(T.sem["tl%d" % q], 16)

    after("v", "ix", "pos")
    did(v.tensor_scalar(T.off[:], T.lst[:], T.pos[:, 0:1], None, A.add), "sv", "off")
    after("v", "off", "row", "low", "vals")
    for t in range(R):
        did(v.tensor_copy(T.row[:, SEG * t:SEG * t + SEG].indirect(T.off[:, 4 * t:4 * t + 4]), T.vals[:, CH * t:CH * t + CH]), "sv", "scat")
    after("v", "wm")
    did(v.quantize_mx(win[:, 0:SH], scl[:, 0:SH], T.wmt[:]), "sv", "base")
    after("v", "dl")
    did(v.quantize_mx(win[:, SH:HELD], scl[:, SH:HELD], T.dlt[:]), "sv", "delta")
    ev["codes%d" % r] = ev["scales%d" % r] = ev["delta"]

    after("v", "scat")
    did(v.transpose(T.tr[:], T.row[:]), "sv", "tr")
    qx(0)
    product(0, r)
    evac("s", 0, r)
    after("v", "tr", "odd", "even")
    did(v.tensor_scalar(T.pa[:], T.tr[:, 0:R * SEG:16], T.even[:, 0:1], None, A.mult), "sv", "pa")
    did(v.tensor_scalar(T.pb[:], T.tr[:, 0:R * SEG:16], T.odd[:, 0:1], None, A.mult), "sv", "pb")
    after("v", "pa", "pb")
    did(v.tensor_tensor(T.gg[:], T.pa[:, 2:54], T.pb[:, 1:53], A.add), "sv", "gg")
    after("v", "gg")
    did(v.tensor_tensor(T.mt[:, 0:16], T.gg[:, 0:16], T.gg[:, 18:34], A.max), "sv", "m2")
    did(v.tensor_tensor(T.nn[:], T.gg[:, 18:34], T.gg[:, 36:52], A.max), "sv", "nn")
    did(v.tensor_scalar(tab[:, 0:16], T.gg[:, 0:16], SH, None, A.add), "sv", "tab1")
    after("v", "nn")
    did(v.tensor_tensor(T.mt[:, 16:32], T.nn[:], T.gg[:, 0:16], A.max), "sv", "m3")
    after("v", "m3")
    did(v.tensor_scalar(tab[:, 16:48], T.mt[:], SH, None, A.add), "sv", "tab")
    for t in (1, 2, 3):
        ev["tab%d_%d" % (r, t)] = ev["tab"]

    send_scales(r, [far1])
    send_scales(r, [near])
    send_codes(r, [near])
    after("y", "tab")
    did(g.sync.dma_start(T.tdram[:], tab[0:16, 16:48]), "tdr", "tdram", 16)
    after("g", "tab")
    send(tab[:], tab[:], "at%d" % r, [near])
    send_codes(r, [far1])
    send(tab[:, 0:16], tab[:, 0:16], "at%d" % r, [far1, far2])
    after("g", "tdram")
    send(T.tdram[:], T["ld%d" % r][:], "ad%d" % r, [far1, far2])
    send_scales(far1, [near])
    send_codes(far1, [near])

    qx(1)
    pick(r, 1, 3)
    product(0, near)
    evac("v", 0, near)
    store(0, hh)
    for t in (1, 2, 3):
        product(t, r)
    pick(near, 1, 2)
    pick(near, 3, 3)
    evac("v", 1, r)
    evac("v", 2, r)
    for t in (1, 2, 3):
        product(t, near)
    evac("s", 3, r)
    repeat(far1)
    repeat(far2)
    pick(far1, 1, 1)
    evac("s", 1, near)
    evac("v", 2, near)
    store(1, hh)
    store(2, hh)
    product(0, far1)
    product(0, far2)
    evac("s", 3, near)
    store(3, hh)
    pick(far2, 1, 1)
    evac("s", 0, far1)
    evac("v", 0, far2)
    store(0, fh)
    product(1, far1)
    product(1, far2)
    pick(far1, 2, 3)
    pick(far2, 2, 2)
    evac("v", 1, far1)
    evac("s", 1, far2)
    store(1, fh)
    product(2, far1)
    product(3, far1)
    pick(far2, 3, 3)
    product(2, far2)
    evac("v", 2, far1)
    product(3, far2)
    evac("s", 2, far2)
    store(2, fh)
    evac("v", 3, far1)
    evac("s", 3, far2)
    store(3, fh)

    g.wait_ge(T.sem["ls"], nls[0])
    after("y", "y")
